import numpy as np
import ml_dtypes


def mxq(x, axis, fmt="e4m3"):
    dtype, down = {"e4m3": (ml_dtypes.float8_e4m3fn, 7), "e5m2": (ml_dtypes.float8_e5m2, 14)}[fmt]
    v = np.moveaxis(np.asarray(x, np.float32).astype(ml_dtypes.bfloat16).astype(np.float64), axis, -1)
    blocks = v.reshape(v.shape[:-1] + (-1, 32))
    amax = np.abs(blocks).max(-1, keepdims=True)
    byte = np.maximum(np.where(amax > 0, np.frexp(amax)[1] - 1 + 127, 0) - down, 1)
    scale = np.exp2(byte - 127.0)
    codes = (blocks / scale).astype(np.float32).astype(dtype).astype(np.float64)
    return np.moveaxis((codes * scale).reshape(v.shape), -1, axis)


WIDE = False


def mx_kscale(k):
    if not WIDE:
        return np.ones(k)
    levels = np.array([30, -30])
    if k % 512:
        return np.exp2(np.random.permutation(np.resize(levels, k // 32))).repeat(32)
    a = np.empty((k // 512, 16))
    for p in range(k // 512):
        a[p, :8] = np.random.permutation(np.resize(levels, 8))
        for g in range(8):
            far = levels[np.abs(levels - a[p, g]) >= 10]
            a[p, g + 8] = far[np.random.randint(len(far))]
    return np.exp2(a.ravel()).repeat(32)


def f64(x):
    return np.asarray(x).astype(np.float64)


def striped(idx):
    return np.tile(np.asarray(idx).reshape(-1, 16).T, (8, 1)).astype(np.uint16)


def unstriped(offs):
    return offs[:16].T.reshape(-1).astype(np.int64)


E2M1 = np.array([0.0, 0.5, 1.0, 1.5, 2.0, 3.0, 4.0, 6.0, -0.0, -0.5, -1.0, -1.5, -2.0, -3.0, -4.0, -6.0])


def pack_weight(w, fmt):
    k, n = w.shape
    w = f64(np.asarray(w, np.float32).astype(ml_dtypes.bfloat16)).reshape(k // 32, 32, n)
    amax = np.abs(w).max(1)
    if fmt in ("e4m3", "e5m2"):
        byte = np.frexp(amax)[1] - 1 + 127 - (7 if fmt == "e4m3" else 14)
    else:
        mant, ex = np.frexp(amax / 6.0)
        byte = np.where(mant > 0.5, ex, ex - 1) + 127
    byte = np.clip(np.where(amax > 0, byte, 1), 1, 254)
    scaled = (w * np.exp2(127.0 - byte)[:, None, :]).reshape(k, n).astype(np.float32)
    by_word = np.ascontiguousarray(scaled.reshape(k // 512, 128, 4, n).transpose(0, 1, 3, 2))
    if fmt in ("e4m3", "e5m2"):
        words = by_word.astype(ml_dtypes.float8_e4m3fn if fmt == "e4m3" else ml_dtypes.float8_e5m2).view(np.uint8)
    else:
        c = by_word.astype(ml_dtypes.float4_e2m1fn).view(np.uint8) & 0xF
        words = (c[..., 0::2] | (c[..., 1::2] << 4)).reshape(k // 512, 128, 2 * n)
    return np.ascontiguousarray(words), np.ascontiguousarray(byte.astype(np.uint8).reshape(k // 512, 16, n))


def unpack_weight(words, scales, fmt):
    g, _, n = scales.shape
    words = np.ascontiguousarray(words).reshape(g, 128, n, -1)
    if fmt in ("e4m3", "e5m2"):
        vals = words.view(ml_dtypes.float8_e4m3fn if fmt == "e4m3" else ml_dtypes.float8_e5m2).astype(np.float64)
    else:
        nib = np.empty((g, 128, n, 4), np.uint8)
        nib[..., 0::2] = words & 0xF
        nib[..., 1::2] = words >> 4
        vals = E2M1[nib]
    vals = vals * np.repeat(np.exp2(scales.astype(np.float64) - 127.0), 8, axis=1)[..., None]
    return vals.transpose(0, 1, 3, 2).reshape(g * 512, n)


def sigmoid(v):
    return 1.0 / (1.0 + np.exp(-v))


def sgn(shape):
    return np.random.uniform(0.5, 2.0, shape) * np.where(np.random.standard_normal(shape) < 0, -1.0, 1.0)


K, T, J, R, O, N, S, E = 512, 1024, 256, 512, 128, 256, 1024, 1024


def setup_inputs():
    n = np.random.standard_normal
    idx = np.random.permutation(T)[:J]
    idx2 = np.random.permutation(J)[:O]
    idx3 = np.random.permutation(J)[:O]
    idx4 = np.random.permutation(S)[:N]
    idx5 = np.random.permutation(E)[:O]
    fk = mx_kscale(K)
    fr = mx_kscale(R)
    xtp = pack_weight(n((K, T)) / fk[:, None], "e2m1")
    wp = pack_weight(n((K, R)) * 1 / np.sqrt(K) * fk[:, None], "e5m2")
    vsp = pack_weight(n((R, S)) * 1 / np.sqrt(R) / fr[:, None], "e4m3")
    return {
        "xt_words": xtp[0],
        "xt_scales": xtp[1],
        "w_words": wp[0],
        "w_scales": wp[1],
        "sa": (np.random.uniform(0.5, 1.6, (R, 1)) * fr[:, None]).astype(np.float32),
        "sg": (sgn((R, 1))).astype(np.float32),
        "bg": (np.random.uniform(-2.0, 2.0, (R, 1))).astype(np.float32),
        "vs_words": vsp[0],
        "vs_scales": vsp[1],
        "offs": striped(idx),
        "offs2": striped(idx2),
        "offs3": striped(idx3),
        "offs4": striped(idx4),
        "offs5": striped(idx5),
    }


def reference(xt_words, xt_scales, w_words, w_scales, sa, sg, bg, vs_words, vs_scales, offs, offs2, offs3, offs4, offs5):
    idx = unstriped(offs)
    idx2 = unstriped(offs2)
    idx3 = unstriped(offs3)
    idx4 = unstriped(offs4)
    idx5 = unstriped(offs5)
    xtu = unpack_weight(xt_words, xt_scales, "e2m1")
    wu = unpack_weight(w_words, w_scales, "e5m2")
    vsu = unpack_weight(vs_words, vs_scales, "e4m3")
    xtidxg = xtu[:, idx]
    a = wu.T @ xtidxg
    hid = a[:, idx2] * f64(sa) * sigmoid(a[:, idx3] * f64(sg) + f64(bg))
    vsidx4g = vsu[:, idx4]
    hidq = mxq(hid, 0, "e5m2")
    p = vsidx4g.T @ hidq
    y = np.zeros((N, E))
    y[:, idx5] = p
    return y

@@ -1,0 +1,181 @@
+from contextlib import ExitStack
+
+import concourse.mybir as mybir
+
+K, T, J, R, O, N, S, E = 512, 1024, 256, 512, 128, 256, 1024, 1024
+FLOPS = 2 * K * R * J + 2 * R * N * O
+
+F32 = mybir.dt.float32
+BF16 = mybir.dt.bfloat16
+I32 = mybir.dt.int32
+U32 = mybir.dt.uint32
+U16 = mybir.dt.uint16
+U8 = mybir.dt.uint8
+E2M1X4 = mybir.dt.float4_e2m1fn_x4
+E5M2X4 = mybir.dt.float8_e5m2_x4
+E4M3X4 = mybir.dt.float8_e4m3fn_x4
+ACT = mybir.ActivationFunctionType
+MULT = mybir.AluOpType.mult
+
+P = 128
+PACK = 4
+QUADS = 4
+QUAD = 32
+ROWS = 4
+LINE = 4
+HALVES = 2
+
+
+def tile_list_gatedpick_solo_store_scattered_kernel(
+    tc, xt_words, xt_scales, w_words, w_scales, sa, sg, bg, vs_words, vs_scales, offs, offs2, offs3, offs4, offs5, out
+):
+    nc = tc.nc
+    with ExitStack() as ctx:
+        lists = ctx.enter_context(tc.tile_pool(name="lists", bufs=1))
+        keep = ctx.enter_context(tc.tile_pool(name="keep", bufs=1))
+        psum = ctx.enter_context(tc.psum_pool(name="psum", bufs=1))
+
+        tok_list = lists.tile([P, J // 16], U16, name="tok_list")
+        val_list = lists.tile([P, O // 16], U16, name="val_list")
+        gate_list = lists.tile([P, O // 16], U16, name="gate_list")
+        entry_list = lists.tile([P, N // 16], U16, name="entry_list")
+        place_list = lists.tile([P, O // 16], U16, name="place_list")
+
+        x_words = keep.tile([P, T], U16, name="x_words", align_bytes=64)
+        x_plane = keep.tile([P, T], U8, name="x_plane", align_bytes=64)
+        w_raw = keep.tile([P, R], I32, name="w_raw", align_bytes=64)
+        w_rows = keep.tile([ROWS, QUADS * R], U8, name="w_rows", align_bytes=64)
+        w_plane = keep.tile([P, R], U8, name="w_plane", align_bytes=64)
+        v_words = keep.tile([P, S], I32, name="v_words", align_bytes=64)
+        v_plane = keep.tile([P, S], U8, name="v_plane", align_bytes=64)
+        sa_t = keep.tile([P, PACK], F32, name="sa_t")
+        sg_t = keep.tile([P, PACK], F32, name="sg_t")
+        bg_t = keep.tile([P, PACK], F32, name="bg_t")
+        pages = [keep.tile([P, E], F32, name=f"page{h}") for h in range(N // P)]
+
+        nc.vector.memset(x_plane[:].bitcast(I32), 0)
+        nc.vector.memset(w_plane[:].bitcast(I32), 0)
+        nc.vector.memset(v_plane[:].bitcast(I32), 0)
+        for page in pages:
+            nc.vector.memset(page[:], 0.0)
+
+        def load_plane(plane, scales):
+            for q in range(QUADS):
+                nc.sync.dma_start(
+                    plane[QUAD * q : QUAD * q + ROWS, :].bitcast(I32),
+                    scales[0, ROWS * q : ROWS * (q + 1), :].bitcast(I32),
+                )
+
+        nc.sync.dma_start(tok_list[:], offs)
+        nc.sync.dma_start(x_words[:].bitcast(I32), xt_words[0].bitcast(I32))
+        nc.scalar.dma_start(
+            w_rows[:].bitcast(I32).rearrange("r (q c) -> r q c", q=QUADS),
+            w_scales[0].bitcast(I32).rearrange("(q r) c -> r q c", r=ROWS),
+        )
+        nc.scalar.dma_start(w_raw[:], w_words[0].rearrange("p c t -> p (c t)").bitcast(I32))
+        load_plane(x_plane, xt_scales)
+        nc.sync.dma_start(gate_list[:], offs3)
+        nc.sync.dma_start(sg_t[:], sg.rearrange("(p t) one -> p (t one)", t=PACK))
+        nc.sync.dma_start(bg_t[:], bg.rearrange("(p t) one -> p (t one)", t=PACK))
+        nc.sync.dma_start(val_list[:], offs2)
+        nc.sync.dma_start(sa_t[:], sa.rearrange("(p t) one -> p (t one)", t=PACK))
+        nc.sync.dma_start(v_words[:], vs_words[0].rearrange("p c t -> p (c t)").bitcast(I32))
+        nc.sync.dma_start(entry_list[:], offs4)
+        load_plane(v_plane, vs_scales)
+        nc.sync.dma_start(place_list[:], offs5)
+
+        w_rows_q = w_rows[:].bitcast(I32).rearrange("r (q c) -> r q c", q=QUADS)
+        for q in range(QUADS):
+            nc.vector.tensor_copy(w_plane[QUAD * q : QUAD * q + ROWS, :].bitcast(I32), w_rows_q[:, q, :])
+        w_dealt = keep.tile([P, R], U32, name="w_dealt", align_bytes=64)
+        w_dealt_plane = keep.tile([P, R], U8, name="w_dealt_plane", align_bytes=64)
+        nc.vector.tensor_copy(
+            w_dealt_plane[:].rearrange("p (t m) -> p m t", t=PACK), w_plane[:].rearrange("p (m t) -> p m t", t=PACK)
+        )
+        nc.scalar.copy(
+            w_dealt[:].rearrange("p (t m) -> p m t", t=PACK),
+            w_raw[:].bitcast(U32).rearrange("p (m t) -> p m t", t=PACK),
+        )
+
+        x_got = keep.tile([P, J], U16, name="x_got", align_bytes=64)
+        x_got_plane = keep.tile([P, J], U8, name="x_got_plane", align_bytes=64)
+        nc.vector.tensor_copy(x_got_plane[:], x_plane[:].indirect(tok_list[:]))
+        nc.vector.tensor_copy(x_got[:], x_words[:].indirect(tok_list[:]))
+
+        gate = keep.tile([P, PACK, O], F32, name="gate")
+        val = keep.tile([P, PACK, O], F32, name="val")
+        for t in range(PACK):
+            cols = slice(P * t, P * (t + 1))
+            a_bank = psum.tile([P, J], F32, name=f"a_bank{t}")
+            nc.tensor.matmul_mx(
+                out=a_bank[:],
+                lhsT=w_dealt[:, cols].bitcast(E5M2X4),
+                lhsT_scale=w_dealt_plane[:, cols],
+                rhs=x_got[:].bitcast(E2M1X4),
+                rhs_scale=x_got_plane[:],
+                start=True,
+                stop=True,
+            )
+            a_rows = keep.tile([P, J], F32, name=f"a_rows{t}")
+            nc.vector.tensor_copy(a_rows[:], a_bank[:])
+            pieces = HALVES if t == PACK - 1 else 1
+            for u in range(pieces):
+                places = slice(u * O // pieces, (u + 1) * O // pieces)
+                entries = slice(places.start // 16, places.stop // 16)
+                nc.scalar.activation(
+                    out=gate[:, t, places],
+                    in_=a_rows[:].indirect(gate_list[:, entries]),
+                    func=ACT.Sigmoid,
+                    bias=bg_t[:, t : t + 1],
+                    scale=sg_t[:, t : t + 1],
+                )
+                nc.scalar.activation(
+                    out=val[:, t, places],
+                    in_=a_rows[:].indirect(val_list[:, entries]),
+                    func=ACT.Copy,
+                    scale=sa_t[:, t : t + 1],
+                )
+
+        v_got = keep.tile([P, N], U32, name="v_got", align_bytes=64)
+        v_got_plane = keep.tile([P, N], U8, name="v_got_plane", align_bytes=64)
+        nc.vector.tensor_copy(v_got[:], v_words[:].bitcast(U32).indirect(entry_list[:]))
+        nc.vector.tensor_copy(v_got_plane[:], v_plane[:].indirect(entry_list[:]))
+
+        hid = keep.tile([P, O, PACK], BF16, name="hid", align_bytes=64)
+        hid_codes = keep.tile([P, O], U32, name="hid_codes", align_bytes=64)
+        hid_plane = keep.tile([P, O], U8, name="hid_plane", align_bytes=64)
+        for u in range(HALVES):
+            places = slice(u * O // HALVES, (u + 1) * O // HALVES)
+            nc.vector.tensor_tensor(
+                hid[:, places, :].rearrange("p (c i) t -> p c t i", i=LINE),
+                val[:, :, places].rearrange("p t (c i) -> p c t i", i=LINE),
+                gate[:, :, places].rearrange("p t (c i) -> p c t i", i=LINE),
+                MULT,
+            )
+            nc.vector.quantize_mx(
+                out=hid_codes[:, places].bitcast(E5M2X4),
+                scales=hid_plane[:, places],
+                in_=hid[:, places, :].rearrange("p o t -> p (o t)"),
+            )
+
+        for h, page in enumerate(pages):
+            cols = slice(P * h, P * (h + 1))
+            p_bank = psum.tile([P, O], F32, name=f"p_bank{h}")
+            nc.tensor.matmul_mx(
+                out=p_bank[:],
+                lhsT=v_got[:, cols].bitcast(E4M3X4),
+                lhsT_scale=v_got_plane[:, cols],
+                rhs=hid_codes[:].bitcast(E5M2X4),
+                rhs_scale=hid_plane[:],
+                start=True,
+                stop=True,
+            )
+            p_rows = keep.tile([P, O], F32, name=f"p_rows{h}")
+            if h == 0:
+                nc.scalar.copy(p_rows[:], p_bank[:])
+                nc.scalar.activation(out=page[:].indirect(place_list[:]), in_=p_rows[:], func=ACT.Copy)
+                nc.scalar.dma_start(out[cols, :], page[:])
+            else:
+                nc.vector.tensor_copy(p_rows[:], p_bank[:])
+                nc.vector.tensor_copy(page[:].indirect(place_list[:]), p_rows[:])
+                nc.sync.dma_start(out[cols, :], page[:])

@@ -24,6 +24,8 @@ QUAD = 32
 ROWS = 4
 LINE = 4
 HALVES = 2
+CUT = 2
+EARLY = 2
 
 
 def tile_list_gatedpick_solo_store_scattered_kernel(
@@ -59,38 +61,39 @@ def tile_list_gatedpick_solo_store_scattered_kernel(
         for page in pages:
             nc.vector.memset(page[:], 0.0)
 
-        def load_plane(plane, scales):
-            for q in range(QUADS):
-                nc.sync.dma_start(
+        def load_plane(plane, scales, queues):
+            for q, queue in enumerate(queues):
+                queue.dma_start(
                     plane[QUAD * q : QUAD * q + ROWS, :].bitcast(I32),
                     scales[0, ROWS * q : ROWS * (q + 1), :].bitcast(I32),
                 )
 
-        nc.sync.dma_start(tok_list[:], offs)
-        nc.sync.dma_start(x_words[:].bitcast(I32), xt_words[0].bitcast(I32))
-        nc.scalar.dma_start(
+        nc.sync.dma_start(
             w_rows[:].bitcast(I32).rearrange("r (q c) -> r q c", q=QUADS),
             w_scales[0].bitcast(I32).rearrange("(q r) c -> r q c", r=ROWS),
         )
-        nc.scalar.dma_start(w_raw[:], w_words[0].rearrange("p c t -> p (c t)").bitcast(I32))
-        load_plane(x_plane, xt_scales)
+        nc.sync.dma_start(tok_list[:], offs)
+        nc.sync.dma_start(x_words[:].bitcast(I32), xt_words[0].bitcast(I32))
+        nc.sync.dma_start(w_raw[:], w_words[0].rearrange("p c t -> p (c t)").bitcast(I32))
+        load_plane(x_plane, xt_scales, [nc.sync, nc.sync, nc.scalar, nc.scalar])
         nc.sync.dma_start(gate_list[:], offs3)
         nc.sync.dma_start(sg_t[:], sg.rearrange("(p t) one -> p (t one)", t=PACK))
         nc.sync.dma_start(bg_t[:], bg.rearrange("(p t) one -> p (t one)", t=PACK))
+        load_plane(v_plane, vs_scales, [nc.sync] * QUADS)
+        nc.sync.dma_start(v_words[:], vs_words[0].rearrange("p c t -> p (c t)").bitcast(I32))
         nc.sync.dma_start(val_list[:], offs2)
         nc.sync.dma_start(sa_t[:], sa.rearrange("(p t) one -> p (t one)", t=PACK))
-        nc.sync.dma_start(v_words[:], vs_words[0].rearrange("p c t -> p (c t)").bitcast(I32))
         nc.sync.dma_start(entry_list[:], offs4)
-        load_plane(v_plane, vs_scales)
         nc.sync.dma_start(place_list[:], offs5)
 
-        w_rows_q = w_rows[:].bitcast(I32).rearrange("r (q c) -> r q c", q=QUADS)
         for q in range(QUADS):
-            nc.vector.tensor_copy(w_plane[QUAD * q : QUAD * q + ROWS, :].bitcast(I32), w_rows_q[:, q, :])
+            nc.vector.tensor_copy(
+                w_plane[QUAD * q : QUAD * q + ROWS, :].bitcast(I32), w_rows[:, R * q : R * (q + 1)].bitcast(I32)
+            )
         w_dealt = keep.tile([P, R], U32, name="w_dealt", align_bytes=64)
         w_dealt_plane = keep.tile([P, R], U8, name="w_dealt_plane", align_bytes=64)
         nc.vector.tensor_copy(
-            w_dealt_plane[:].rearrange("p (t m) -> p m t", t=PACK), w_plane[:].rearrange("p (m t) -> p m t", t=PACK)
+            w_dealt_plane[:].rearrange("p (t m) -> p t m", t=PACK), w_plane[:].rearrange("p (m t) -> p t m", t=PACK)
         )
         nc.scalar.copy(
             w_dealt[:].rearrange("p (t m) -> p m t", t=PACK),
@@ -99,42 +102,60 @@ def tile_list_gatedpick_solo_store_scattered_kernel(
 
         x_got = keep.tile([P, J], U16, name="x_got", align_bytes=64)
         x_got_plane = keep.tile([P, J], U8, name="x_got_plane", align_bytes=64)
-        nc.vector.tensor_copy(x_got_plane[:], x_plane[:].indirect(tok_list[:]))
+        first, second = slice(0, J // HALVES), slice(J // HALVES, J)
         nc.vector.tensor_copy(x_got[:], x_words[:].indirect(tok_list[:]))
+        for slots in (first, second):
+            nc.vector.tensor_copy(
+                x_got_plane[:, slots], x_plane[:].indirect(tok_list[:, slots.start // 16 : slots.stop // 16])
+            )
 
-        gate = keep.tile([P, PACK, O], F32, name="gate")
-        val = keep.tile([P, PACK, O], F32, name="val")
-        for t in range(PACK):
+        a_tiles = [keep.tile([P, J], F32, name=f"a_rows{t}") for t in range(PACK)]
+
+        def first_product(t, slots, copy_out):
             cols = slice(P * t, P * (t + 1))
-            a_bank = psum.tile([P, J], F32, name=f"a_bank{t}")
+            a_bank = psum.tile([P, slots.stop - slots.start], F32, name=f"a_bank{t}_{slots.start}")
             nc.tensor.matmul_mx(
                 out=a_bank[:],
                 lhsT=w_dealt[:, cols].bitcast(E5M2X4),
                 lhsT_scale=w_dealt_plane[:, cols],
-                rhs=x_got[:].bitcast(E2M1X4),
-                rhs_scale=x_got_plane[:],
+                rhs=x_got[:, slots].bitcast(E2M1X4),
+                rhs_scale=x_got_plane[:, slots],
                 start=True,
                 stop=True,
             )
-            a_rows = keep.tile([P, J], F32, name=f"a_rows{t}")
-            nc.vector.tensor_copy(a_rows[:], a_bank[:])
-            pieces = HALVES if t == PACK - 1 else 1
-            for u in range(pieces):
-                places = slice(u * O // pieces, (u + 1) * O // pieces)
-                entries = slice(places.start // 16, places.stop // 16)
-                nc.scalar.activation(
-                    out=gate[:, t, places],
-                    in_=a_rows[:].indirect(gate_list[:, entries]),
-                    func=ACT.Sigmoid,
-                    bias=bg_t[:, t : t + 1],
-                    scale=sg_t[:, t : t + 1],
-                )
-                nc.scalar.activation(
-                    out=val[:, t, places],
-                    in_=a_rows[:].indirect(val_list[:, entries]),
-                    func=ACT.Copy,
-                    scale=sa_t[:, t : t + 1],
-                )
+            copy_out(a_tiles[t][:, slots], a_bank[:])
+
+        for t in range(EARLY):
+            first_product(t, first, nc.scalar.copy)
+        for t in range(EARLY):
+            first_product(t, second, nc.vector.tensor_copy)
+        for t in range(EARLY, PACK):
+            first_product(t, slice(0, J), nc.vector.tensor_copy)
+
+        gate = keep.tile([P, PACK, O], F32, name="gate")
+        val = keep.tile([P, PACK, O], F32, name="val")
+        for t in range(PACK):
+            nc.scalar.activation(
+                out=gate[:, t, :],
+                in_=a_tiles[t][:].indirect(gate_list[:]),
+                func=ACT.Sigmoid,
+                bias=bg_t[:, t : t + 1],
+                scale=sg_t[:, t : t + 1],
+            )
+
+        def fetch_values(t, places):
+            nc.scalar.activation(
+                out=val[:, t, places],
+                in_=a_tiles[t][:].indirect(val_list[:, places.start // 16 : places.stop // 16]),
+                func=ACT.Copy,
+                scale=sa_t[:, t : t + 1],
+            )
+
+        for t in range(PACK - CUT):
+            fetch_values(t, slice(0, O))
+        for u in range(HALVES):
+            for t in range(PACK - CUT, PACK):
+                fetch_values(t, slice(u * O // HALVES, (u + 1) * O // HALVES))
 
         v_got = keep.tile([P, N], U32, name="v_got", align_bytes=64)
         v_got_plane = keep.tile([P, N], U8, name="v_got_plane", align_bytes=64)

@@ -56,6 +56,9 @@ def tile_list_gatedpick_solo_store_scattered_kernel(
         pages = [keep.tile([P, E], F32, name=f"page{h}") for h in range(N // P)]
 
         nc.vector.memset(x_plane[:].bitcast(I32), 0)
+        warm_in = keep.tile([P, 1], F32, name="warm_in")
+        warm_out = keep.tile([P, 1], F32, name="warm_out")
+        nc.vector.memset(warm_in[:], 0.0)
         nc.vector.memset(w_plane[:].bitcast(I32), 0)
         nc.vector.memset(v_plane[:].bitcast(I32), 0)
         for page in pages:
@@ -76,6 +79,7 @@ def tile_list_gatedpick_solo_store_scattered_kernel(
         nc.sync.dma_start(x_words[:].bitcast(I32), xt_words[0].bitcast(I32))
         nc.sync.dma_start(w_raw[:], w_words[0].rearrange("p c t -> p (c t)").bitcast(I32))
         load_plane(x_plane, xt_scales, [nc.sync, nc.sync, nc.scalar, nc.scalar])
+        nc.scalar.activation(out=warm_out[:], in_=warm_in[:], func=ACT.Sigmoid)
         nc.sync.dma_start(gate_list[:], offs3)
         nc.sync.dma_start(sg_t[:], sg.rearrange("(p t) one -> p (t one)", t=PACK))
         nc.sync.dma_start(bg_t[:], bg.rearrange("(p t) one -> p (t one)", t=PACK))

@@ -49,11 +49,11 @@ def tile_list_gatedpick_solo_store_scattered_kernel(
         w_rows = keep.tile([ROWS, QUADS * R], U8, name="w_rows", align_bytes=64)
         w_plane = keep.tile([P, R], U8, name="w_plane", align_bytes=64)
         v_words = keep.tile([P, S], I32, name="v_words", align_bytes=64)
-        v_plane = keep.tile([P, S], U8, name="v_plane", align_bytes=64)
+        v_plane = keep.tile([P, S], U8, name="v_plane", tag="v_plane_then_hid", align_bytes=64)
         sa_t = keep.tile([P, PACK], F32, name="sa_t")
         sg_t = keep.tile([P, PACK], F32, name="sg_t")
         bg_t = keep.tile([P, PACK], F32, name="bg_t")
-        pages = [keep.tile([P, E], F32, name=f"page{h}") for h in range(N // P)]
+        page0 = keep.tile([P, E], F32, name="page0")
 
         nc.vector.memset(x_plane[:].bitcast(I32), 0)
         warm_in = keep.tile([P, 1], F32, name="warm_in")
@@ -61,8 +61,7 @@ def tile_list_gatedpick_solo_store_scattered_kernel(
         nc.vector.memset(warm_in[:], 0.0)
         nc.vector.memset(w_plane[:].bitcast(I32), 0)
         nc.vector.memset(v_plane[:].bitcast(I32), 0)
-        for page in pages:
-            nc.vector.memset(page[:], 0.0)
+        nc.vector.memset(page0[:], 0.0)
 
         def load_plane(plane, scales, queues):
             for q, queue in enumerate(queues):
@@ -83,18 +82,18 @@ def tile_list_gatedpick_solo_store_scattered_kernel(
         nc.sync.dma_start(gate_list[:], offs3)
         nc.sync.dma_start(sg_t[:], sg.rearrange("(p t) one -> p (t one)", t=PACK))
         nc.sync.dma_start(bg_t[:], bg.rearrange("(p t) one -> p (t one)", t=PACK))
-        load_plane(v_plane, vs_scales, [nc.sync] * QUADS)
-        nc.sync.dma_start(v_words[:], vs_words[0].rearrange("p c t -> p (c t)").bitcast(I32))
         nc.sync.dma_start(val_list[:], offs2)
         nc.sync.dma_start(sa_t[:], sa.rearrange("(p t) one -> p (t one)", t=PACK))
+        nc.sync.dma_start(v_words[:], vs_words[0].rearrange("p c t -> p (c t)").bitcast(I32))
         nc.sync.dma_start(entry_list[:], offs4)
+        load_plane(v_plane, vs_scales, [nc.sync] * QUADS)
         nc.sync.dma_start(place_list[:], offs5)
 
         for q in range(QUADS):
             nc.vector.tensor_copy(
                 w_plane[QUAD * q : QUAD * q + ROWS, :].bitcast(I32), w_rows[:, R * q : R * (q + 1)].bitcast(I32)
             )
-        w_dealt = keep.tile([P, R], U32, name="w_dealt", align_bytes=64)
+        w_dealt = keep.tile([P, R], U32, name="w_dealt", tag="w_dealt_then_page1", align_bytes=64)
         w_dealt_plane = keep.tile([P, R], U8, name="w_dealt_plane", align_bytes=64)
         nc.vector.tensor_copy(
             w_dealt_plane[:].rearrange("p (t m) -> p t m", t=PACK), w_plane[:].rearrange("p (m t) -> p t m", t=PACK)
@@ -166,7 +165,10 @@ def tile_list_gatedpick_solo_store_scattered_kernel(
         nc.vector.tensor_copy(v_got[:], v_words[:].bitcast(U32).indirect(entry_list[:]))
         nc.vector.tensor_copy(v_got_plane[:], v_plane[:].indirect(entry_list[:]))
 
-        hid = keep.tile([P, O, PACK], BF16, name="hid", align_bytes=64)
+        page1 = keep.tile([P, E], F32, name="page1", tag="w_dealt_then_page1", align_bytes=64)
+        nc.gpsimd.memset(page1[:], 0.0)
+
+        hid = keep.tile([P, O, PACK], BF16, name="hid", tag="v_plane_then_hid", align_bytes=64)
         hid_codes = keep.tile([P, O], U32, name="hid_codes", align_bytes=64)
         hid_plane = keep.tile([P, O], U8, name="hid_plane", align_bytes=64)
         for u in range(HALVES):
@@ -183,7 +185,7 @@ def tile_list_gatedpick_solo_store_scattered_kernel(
                 in_=hid[:, places, :].rearrange("p o t -> p (o t)"),
             )
 
-        for h, page in enumerate(pages):
+        for h, page in enumerate((page0, page1)):
             cols = slice(P * h, P * (h + 1))
             p_bank = psum.tile([P, O], F32, name=f"p_bank{h}")
             nc.tensor.matmul_mx(

@@ -95,7 +95,7 @@ def tile_list_gatedpick_solo_store_scattered_kernel(
             )
         w_dealt = keep.tile([P, R], U32, name="w_dealt", tag="w_dealt_then_page1", align_bytes=64)
         w_dealt_plane = keep.tile([P, R], U8, name="w_dealt_plane", align_bytes=64)
-        nc.vector.tensor_copy(
+        nc.gpsimd.tensor_copy(
             w_dealt_plane[:].rearrange("p (t m) -> p t m", t=PACK), w_plane[:].rearrange("p (m t) -> p t m", t=PACK)
         )
         nc.scalar.copy(

from contextlib import ExitStack

import concourse.mybir as mybir

K, T, J, R, O, N, S, E = 512, 1024, 256, 512, 128, 256, 1024, 1024
FLOPS = 2 * K * R * J + 2 * R * N * O

F32 = mybir.dt.float32
BF16 = mybir.dt.bfloat16
I32 = mybir.dt.int32
U32 = mybir.dt.uint32
U16 = mybir.dt.uint16
U8 = mybir.dt.uint8
E2M1X4 = mybir.dt.float4_e2m1fn_x4
E5M2X4 = mybir.dt.float8_e5m2_x4
E4M3X4 = mybir.dt.float8_e4m3fn_x4
ACT = mybir.ActivationFunctionType
MULT = mybir.AluOpType.mult

P = 128
PACK = 4
QUADS = 4
QUAD = 32
ROWS = 4
LINE = 4
HALVES = 2
CUT = 2
EARLY = 2


def tile_list_gatedpick_solo_store_scattered_kernel(
    tc, xt_words, xt_scales, w_words, w_scales, sa, sg, bg, vs_words, vs_scales, offs, offs2, offs3, offs4, offs5, out
):
    nc = tc.nc
    with ExitStack() as ctx:
        lists = ctx.enter_context(tc.tile_pool(name="lists", bufs=1))
        keep = ctx.enter_context(tc.tile_pool(name="keep", bufs=1))
        psum = ctx.enter_context(tc.psum_pool(name="psum", bufs=1))

        tok_list = lists.tile([P, J // 16], U16, name="tok_list")
        val_list = lists.tile([P, O // 16], U16, name="val_list")
        gate_list = lists.tile([P, O // 16], U16, name="gate_list")
        entry_list = lists.tile([P, N // 16], U16, name="entry_list")
        place_list = lists.tile([P, O // 16], U16, name="place_list")

        x_words = keep.tile([P, T], U16, name="x_words", align_bytes=64)
        x_plane = keep.tile([P, T], U8, name="x_plane", align_bytes=64)
        w_raw = keep.tile([P, R], I32, name="w_raw", align_bytes=64)
        w_rows = keep.tile([ROWS, QUADS * R], U8, name="w_rows", align_bytes=64)
        w_plane = keep.tile([P, R], U8, name="w_plane", align_bytes=64)
        v_words = keep.tile([P, S], I32, name="v_words", align_bytes=64)
        v_plane = keep.tile([P, S], U8, name="v_plane", tag="v_plane_then_hid", align_bytes=64)
        sa_t = keep.tile([P, PACK], F32, name="sa_t")
        sg_t = keep.tile([P, PACK], F32, name="sg_t")
        bg_t = keep.tile([P, PACK], F32, name="bg_t")
        page0 = keep.tile([P, E], F32, name="page0")

        nc.vector.memset(x_plane[:].bitcast(I32), 0)
        warm_in = keep.tile([P, 1], F32, name="warm_in")
        warm_out = keep.tile([P, 1], F32, name="warm_out")
        nc.vector.memset(warm_in[:], 0.0)
        nc.vector.memset(w_plane[:].bitcast(I32), 0)
        nc.vector.memset(v_plane[:].bitcast(I32), 0)
        nc.vector.memset(page0[:], 0.0)

        def load_plane(plane, scales, queues):
            for q, queue in enumerate(queues):
                queue.dma_start(
                    plane[QUAD * q : QUAD * q + ROWS, :].bitcast(I32),
                    scales[0, ROWS * q : ROWS * (q + 1), :].bitcast(I32),
                )

        nc.sync.dma_start(
            w_rows[:].bitcast(I32).rearrange("r (q c) -> r q c", q=QUADS),
            w_scales[0].bitcast(I32).rearrange("(q r) c -> r q c", r=ROWS),
        )
        nc.sync.dma_start(tok_list[:], offs)
        nc.sync.dma_start(x_words[:].bitcast(I32), xt_words[0].bitcast(I32))
        nc.sync.dma_start(w_raw[:], w_words[0].rearrange("p c t -> p (c t)").bitcast(I32))
        load_plane(x_plane, xt_scales, [nc.sync, nc.sync, nc.scalar, nc.scalar])
        nc.scalar.activation(out=warm_out[:], in_=warm_in[:], func=ACT.Sigmoid)
        nc.sync.dma_start(gate_list[:], offs3)
        nc.sync.dma_start(sg_t[:], sg.rearrange("(p t) one -> p (t one)", t=PACK))
        nc.sync.dma_start(bg_t[:], bg.rearrange("(p t) one -> p (t one)", t=PACK))
        nc.sync.dma_start(val_list[:], offs2)
        nc.sync.dma_start(sa_t[:], sa.rearrange("(p t) one -> p (t one)", t=PACK))
        nc.sync.dma_start(v_words[:], vs_words[0].rearrange("p c t -> p (c t)").bitcast(I32))
        nc.sync.dma_start(entry_list[:], offs4)
        load_plane(v_plane, vs_scales, [nc.sync] * QUADS)
        nc.sync.dma_start(place_list[:], offs5)

        for q in range(QUADS):
            nc.vector.tensor_copy(
                w_plane[QUAD * q : QUAD * q + ROWS, :].bitcast(I32), w_rows[:, R * q : R * (q + 1)].bitcast(I32)
            )
        w_dealt = keep.tile([P, R], U32, name="w_dealt", tag="w_dealt_then_page1", align_bytes=64)
        w_dealt_plane = keep.tile([P, R], U8, name="w_dealt_plane", align_bytes=64)
        nc.gpsimd.tensor_copy(
            w_dealt_plane[:].rearrange("p (t m) -> p t m", t=PACK), w_plane[:].rearrange("p (m t) -> p t m", t=PACK)
        )
        nc.scalar.copy(
            w_dealt[:].rearrange("p (t m) -> p m t", t=PACK),
            w_raw[:].bitcast(U32).rearrange("p (m t) -> p m t", t=PACK),
        )

        x_got = keep.tile([P, J], U16, name="x_got", align_bytes=64)
        x_got_plane = keep.tile([P, J], U8, name="x_got_plane", align_bytes=64)
        first, second = slice(0, J // HALVES), slice(J // HALVES, J)
        nc.vector.tensor_copy(x_got[:], x_words[:].indirect(tok_list[:]))
        for slots in (first, second):
            nc.vector.tensor_copy(
                x_got_plane[:, slots], x_plane[:].indirect(tok_list[:, slots.start // 16 : slots.stop // 16])
            )

        a_tiles = [keep.tile([P, J], F32, name=f"a_rows{t}") for t in range(PACK)]

        def first_product(t, slots, copy_out):
            cols = slice(P * t, P * (t + 1))
            a_bank = psum.tile([P, slots.stop - slots.start], F32, name=f"a_bank{t}_{slots.start}")
            nc.tensor.matmul_mx(
                out=a_bank[:],
                lhsT=w_dealt[:, cols].bitcast(E5M2X4),
                lhsT_scale=w_dealt_plane[:, cols],
                rhs=x_got[:, slots].bitcast(E2M1X4),
                rhs_scale=x_got_plane[:, slots],
                start=True,
                stop=True,
            )
            copy_out(a_tiles[t][:, slots], a_bank[:])

        for t in range(EARLY):
            first_product(t, first, nc.scalar.copy)
        for t in range(EARLY):
            first_product(t, second, nc.vector.tensor_copy)
        for t in range(EARLY, PACK):
            first_product(t, slice(0, J), nc.vector.tensor_copy)

        gate = keep.tile([P, PACK, O], F32, name="gate")
        val = keep.tile([P, PACK, O], F32, name="val")
        for t in range(PACK):
            nc.scalar.activation(
                out=gate[:, t, :],
                in_=a_tiles[t][:].indirect(gate_list[:]),
                func=ACT.Sigmoid,
                bias=bg_t[:, t : t + 1],
                scale=sg_t[:, t : t + 1],
            )

        def fetch_values(t, places):
            nc.scalar.activation(
                out=val[:, t, places],
                in_=a_tiles[t][:].indirect(val_list[:, places.start // 16 : places.stop // 16]),
                func=ACT.Copy,
                scale=sa_t[:, t : t + 1],
            )

        for t in range(PACK - CUT):
            fetch_values(t, slice(0, O))
        for u in range(HALVES):
            for t in range(PACK - CUT, PACK):
                fetch_values(t, slice(u * O // HALVES, (u + 1) * O // HALVES))

        v_got = keep.tile([P, N], U32, name="v_got", align_bytes=64)
        v_got_plane = keep.tile([P, N], U8, name="v_got_plane", align_bytes=64)
        nc.vector.tensor_copy(v_got[:], v_words[:].bitcast(U32).indirect(entry_list[:]))
        nc.vector.tensor_copy(v_got_plane[:], v_plane[:].indirect(entry_list[:]))

        page1 = keep.tile([P, E], F32, name="page1", tag="w_dealt_then_page1", align_bytes=64)
        nc.gpsimd.memset(page1[:], 0.0)

        hid = keep.tile([P, O, PACK], BF16, name="hid", tag="v_plane_then_hid", align_bytes=64)
        hid_codes = keep.tile([P, O], U32, name="hid_codes", align_bytes=64)
        hid_plane = keep.tile([P, O], U8, name="hid_plane", align_bytes=64)
        for u in range(HALVES):
            places = slice(u * O // HALVES, (u + 1) * O // HALVES)
            nc.vector.tensor_tensor(
                hid[:, places, :].rearrange("p (c i) t -> p c t i", i=LINE),
                val[:, :, places].rearrange("p t (c i) -> p c t i", i=LINE),
                gate[:, :, places].rearrange("p t (c i) -> p c t i", i=LINE),
                MULT,
            )
            nc.vector.quantize_mx(
                out=hid_codes[:, places].bitcast(E5M2X4),
                scales=hid_plane[:, places],
                in_=hid[:, places, :].rearrange("p o t -> p (o t)"),
            )

        for h, page in enumerate((page0, page1)):
            cols = slice(P * h, P * (h + 1))
            p_bank = psum.tile([P, O], F32, name=f"p_bank{h}")
            nc.tensor.matmul_mx(
                out=p_bank[:],
                lhsT=v_got[:, cols].bitcast(E4M3X4),
                lhsT_scale=v_got_plane[:, cols],
                rhs=hid_codes[:].bitcast(E5M2X4),
                rhs_scale=hid_plane[:],
                start=True,
                stop=True,
            )
            p_rows = keep.tile([P, O], F32, name=f"p_rows{h}")
            if h == 0:
                nc.scalar.copy(p_rows[:], p_bank[:])
                nc.scalar.activation(out=page[:].indirect(place_list[:]), in_=p_rows[:], func=ACT.Copy)
                nc.scalar.dma_start(out[cols, :], page[:])
            else:
                nc.vector.tensor_copy(p_rows[:], p_bank[:])
                nc.vector.tensor_copy(page[:].indirect(place_list[:]), p_rows[:])
                nc.sync.dma_start(out[cols, :], page[:])
